import numpy as np
import ml_dtypes


def mxq(x, axis, fmt="e4m3"):
    dtype, down = {"e4m3": (ml_dtypes.float8_e4m3fn, 7), "e5m2": (ml_dtypes.float8_e5m2, 14)}[fmt]
    v = np.moveaxis(np.asarray(x, np.float32).astype(ml_dtypes.bfloat16).astype(np.float64), axis, -1)
    blocks = v.reshape(v.shape[:-1] + (-1, 32))
    amax = np.abs(blocks).max(-1, keepdims=True)
    byte = np.maximum(np.where(amax > 0, np.frexp(amax)[1] - 1 + 127, 0) - down, 1)
    scale = np.exp2(byte - 127.0)
    codes = (blocks / scale).astype(np.float32).astype(dtype).astype(np.float64)
    return np.moveaxis((codes * scale).reshape(v.shape), -1, axis)


WIDE = False


def mx_kscale(k):
    if not WIDE:
        return np.ones(k)
    levels = np.array([10, -10, 5, -5, 0])
    if k % 512:
        return np.exp2(np.random.permutation(np.resize(levels, k // 32))).repeat(32)
    a = np.empty((k // 512, 16))
    for p in range(k // 512):
        a[p, :8] = np.random.permutation(np.resize(levels, 8))
        for g in range(8):
            far = levels[np.abs(levels - a[p, g]) >= 10]
            a[p, g + 8] = far[np.random.randint(len(far))]
    return np.exp2(a.ravel()).repeat(32)


def f64(x):
    return np.asarray(x).astype(np.float64)


def striped8(idx):
    return np.concatenate([v.reshape(-1, 16).T for v in idx]).astype(np.uint16)


def unstriped8(offs):
    return np.stack([offs[16 * g:16 * g + 16].T.reshape(-1) for g in range(8)]).astype(np.int64)


E2M1 = np.array([0.0, 0.5, 1.0, 1.5, 2.0, 3.0, 4.0, 6.0, -0.0, -0.5, -1.0, -1.5, -2.0, -3.0, -4.0, -6.0])


def pack_weight(w, fmt):
    k, n = w.shape
    w = f64(np.asarray(w, np.float32).astype(ml_dtypes.bfloat16)).reshape(k // 32, 32, n)
    amax = np.abs(w).max(1)
    if fmt == "e4m3":
        byte = np.frexp(amax)[1] - 1 + 127 - 7
    else:
        mant, ex = np.frexp(amax / 6.0)
        byte = np.where(mant > 0.5, ex, ex - 1) + 127
    byte = np.clip(np.where(amax > 0, byte, 1), 1, 254)
    scaled = (w * np.exp2(127.0 - byte)[:, None, :]).reshape(k, n).astype(np.float32)
    by_word = np.ascontiguousarray(scaled.reshape(k // 512, 128, 4, n).transpose(0, 1, 3, 2))
    if fmt == "e4m3":
        words = by_word.astype(ml_dtypes.float8_e4m3fn).view(np.uint8)
    else:
        c = by_word.astype(ml_dtypes.float4_e2m1fn).view(np.uint8) & 0xF
        words = (c[..., 0::2] | (c[..., 1::2] << 4)).reshape(k // 512, 128, 2 * n)
    return np.ascontiguousarray(words), np.ascontiguousarray(byte.astype(np.uint8).reshape(k // 512, 16, n))


def unpack_weight(words, scales, fmt):
    g, _, n = scales.shape
    words = np.ascontiguousarray(words).reshape(g, 128, n, -1)
    if fmt == "e4m3":
        vals = words.view(ml_dtypes.float8_e4m3fn).astype(np.float64)
    else:
        nib = np.empty((g, 128, n, 4), np.uint8)
        nib[..., 0::2] = words & 0xF
        nib[..., 1::2] = words >> 4
        vals = E2M1[nib]
    vals = vals * np.repeat(np.exp2(scales.astype(np.float64) - 127.0), 8, axis=1)[..., None]
    return vals.transpose(0, 1, 3, 2).reshape(g * 512, n)


def silu(v):
    return v / (1.0 + np.exp(-np.maximum(v, -700.0)))


K, M, T, S = 1536, 1024, 1024, 512


def setup_inputs():
    n = np.random.standard_normal
    s = mx_kscale(K)[:, None]
    u = mx_kscale(512)[:, None]
    p_w4 = pack_weight(n((K, M)) / np.sqrt(K) / s, "e2m1")
    return {
        "xT": (n((K, T)) * s).astype(np.float32),
        "w4_words": p_w4[0],
        "w4_scales": p_w4[1],
        "down": (n((K, 512)) / np.sqrt(K) / s * u.T).astype(np.float32),
        "up": (0.5 * n((512, M)) / np.sqrt(512) / u).astype(np.float32),
        "wgt": np.repeat(np.random.uniform(0.5, 2.0, (8, S)), 16, axis=0).astype(np.float32),
        "b": (0.3 * n(1024)).astype(np.float32),
        "wgo": np.repeat(np.random.uniform(0.5, 2.0, (8, S)), 16, axis=0).astype(np.float32),
        "offs": striped8(np.stack([np.random.permutation(T)[:S] for _ in range(8)])),
        "offs2": striped8(np.stack([np.random.permutation(T)[:S] for _ in range(8)])),
    }


def reference(xT, w4_words, w4_scales, down, up, wgt, b, wgo, offs, offs2):
    idx = unstriped8(offs)
    group = np.arange(K) % 512 // 64
    xg = f64(wgt)[np.arange(K) // 4 % 128] * f64(xT)[np.arange(K)[:, None], idx[group]]
    xT_ = mxq(xg, 0, "e4m3")
    w4_ = unpack_weight(w4_words, w4_scales, "e2m1")
    down_ = mxq(f64(down), 0, "e4m3")
    up_ = mxq(f64(up), 0, "e4m3")
    h_ = mxq(down_.T @ xT_, 0, "e4m3")
    y = w4_.T @ xT_ + up_.T @ h_
    place = unstriped8(offs2)[np.arange(M) % 128 // 16]
    out = np.zeros((M, T))
    out[np.arange(M)[:, None], place] = f64(wgo)[np.arange(M) % 128] * (silu(y + f64(b)[:, None]))
    return out

@@ -1,0 +1,274 @@
+from contextlib import ExitStack
+
+import concourse.mybir as mybir
+from concourse.masks import make_identity
+
+K, M, T, S, R = 1536, 1024, 1024, 512, 512
+FLOPS = 2 * S * (K * M + K * R + R * M)
+
+F32 = mybir.dt.float32
+BF16 = mybir.dt.bfloat16
+I32 = mybir.dt.int32
+U32 = mybir.dt.uint32
+U16 = mybir.dt.uint16
+U8 = mybir.dt.uint8
+FP8X4 = mybir.dt.float8_e4m3fn_x4
+FP4X4 = mybir.dt.float4_e2m1fn_x4
+MULT = mybir.AluOpType.mult
+SILU = mybir.ActivationFunctionType.Silu
+
+P = 128
+PACK = 4
+K_PASS = P * PACK
+PASSES = K // K_PASS
+LAST = PASSES - 1
+TILES = M // P
+CHUNK = 128
+CHUNKS = S // CHUNK
+GROUP = 16
+WINDOWS = 4
+UP_PIECES = ((0, 1), (1, 2), (2, 4), (4, 8))
+
+
+def tile_list_hboth_l_silu_kernel(
+    tc, xT, w4_words, w4_scales, down, up, wgt, b, wgo, offs, offs2, out
+):
+    nc = tc.nc
+
+    with ExitStack() as ctx:
+        held = ctx.enter_context(tc.tile_pool(name="held", bufs=1))
+        ring = ctx.enter_context(tc.tile_pool(name="ring", bufs=2))
+        acts = ctx.enter_context(tc.tile_pool(name="acts", bufs=3))
+        h_psum = ctx.enter_context(tc.psum_pool(name="h_psum", bufs=1))
+        y_psum = ctx.enter_context(tc.psum_pool(name="y_psum", bufs=4))
+
+        def mx_operand(name, width):
+            codes = held.tile([P, width], U32, name=name + "_codes", align_bytes=64)
+            scales = held.tile([P, width], U8, name=name + "_scales", align_bytes=64)
+            return codes, scales
+
+        def quantize(operand, cols, grouped):
+            codes, scales = operand
+            nc.vector.quantize_mx(out=codes[:, cols].bitcast(FP8X4), scales=scales[:, cols], in_=grouped)
+
+        def interleave(copy, grouped, rows):
+            copy(
+                grouped.rearrange("p (c i t) -> p c t i", i=4, t=PACK),
+                rows.rearrange("p t (c i) -> p c t i", i=4),
+            )
+
+        def chunk_cols(c):
+            return slice(c * CHUNK, (c + 1) * CHUNK)
+
+        def chunk_offsets(c):
+            return slice(c * CHUNK // GROUP, (c + 1) * CHUNK // GROUP)
+
+        picks = held.tile([P, S // GROUP], U16, name="picks")
+        places = held.tile([P, S // GROUP], U16, name="places")
+        wgt_sb = held.tile([P, S], F32, name="wgt_sb")
+        wgo_sb = held.tile([P, S], F32, name="wgo_sb")
+        nc.sync.dma_start(picks[:], offs)
+        nc.sync.dma_start(wgt_sb[:], wgt)
+
+        windows = [held.tile([P, T], F32, name="window%d" % w) for w in range(WINDOWS)]
+        for window in windows:
+            nc.vector.memset(window[:], 0.0)
+        w4_scale = held.tile([P, PASSES, M], U8, name="w4_scale", align_bytes=64)
+        nc.vector.memset(w4_scale[:].bitcast(I32), 0)
+
+        ident = held.tile([P, P], F32, name="ident")
+        make_identity(nc, ident[:])
+        b_rows = held.tile([P, P], F32, name="b_rows")
+        nc.scalar.activation(b_rows[:], ident[:], SILU, scale=0.0)
+
+        xg = [mx_operand("xg%d" % a, S) for a in range(PASSES)]
+        dn = [mx_operand("down%d" % a, R) for a in range(PASSES)]
+        hq = mx_operand("h", S)
+        h_banks = [h_psum.tile([P, PACK, CHUNK], F32, name="h_bank%d" % c) for c in range(CHUNKS)]
+
+        def load_x(a):
+            rows = xT[a * K_PASS : (a + 1) * K_PASS, :].rearrange("(p i) t -> p i t", i=PACK)
+            planes = []
+            for i in range(PACK):
+                plane = held.tile([P, T], F32, name="x%d_%d" % (a, i))
+                nc.sync.dma_start(plane[:], rows[:, i, :])
+                planes.append(plane)
+            return planes
+
+        def load_down(a):
+            raw = held.tile([P, PACK, R], F32, name="down_raw%d" % a)
+            nc.sync.dma_start(raw[:], down[a * K_PASS : (a + 1) * K_PASS, :].rearrange("(p j) r -> p j r", j=PACK))
+            return raw
+
+        def gather(picked, i, plane):
+            nc.vector.tensor_tensor(picked[:, i, :], plane[:].indirect(picks[:]), wgt_sb[:], MULT)
+
+        def make_xg(a, planes):
+            picked = ring.tile([P, PACK, S], F32, name="picked")
+            for i in range(PACK):
+                gather(picked, i, planes[i])
+            grouped = ring.tile([P, S * PACK], BF16, name="xg_grouped", align_bytes=64)
+            interleave(nc.scalar.copy, grouped[:], picked[:])
+            quantize(xg[a], slice(0, S), grouped[:])
+
+        def make_down(a, raw):
+            grouped = ring.tile([P, R * PACK], BF16, name="down_grouped", align_bytes=64)
+            nc.scalar.copy(
+                grouped[:].rearrange("p (t m j) -> p m j t", t=PACK, j=PACK),
+                raw[:].rearrange("p j (m t) -> p m j t", t=PACK),
+            )
+            quantize(dn[a], slice(0, R), grouped[:])
+
+        def h_pass(a, c, t):
+            nc.tensor.matmul_mx(
+                out=h_banks[c][:, t, :],
+                lhsT=dn[a][0][:, t * P : (t + 1) * P].bitcast(FP8X4),
+                lhsT_scale=dn[a][1][:, t * P : (t + 1) * P],
+                rhs=xg[a][0][:, chunk_cols(c)].bitcast(FP8X4),
+                rhs_scale=xg[a][1][:, chunk_cols(c)],
+                start=(a == 0 and t == 0),
+                stop=(a == LAST and t == PACK - 1),
+            )
+
+        def h_passes(a):
+            for t in range(PACK):
+                for c in range(CHUNKS):
+                    h_pass(a, c, t)
+
+        x0 = load_x(0)
+        d0 = load_down(0)
+        d1 = load_down(1)
+        x1 = load_x(1)
+        d2 = load_down(2)
+        nc.sync.dma_start(b_rows[0:TILES, :], b.rearrange("(i p) -> i p", p=P))
+        x2 = load_x(2)
+
+        scale_rows = w4_scales.rearrange("a q n -> q a n")
+        for q in range(4):
+            nc.sync.dma_start(
+                w4_scale[32 * q : 32 * q + 4, :, :].bitcast(I32), scale_rows[4 * q : 4 * q + 4, :, :].bitcast(I32)
+            )
+        word_rows = w4_words.rearrange("a p n -> p a n")
+        w4_first = held.tile([P, PASSES, 2 * P], U8, name="w4_first", align_bytes=64)
+        w4_rest = held.tile([P, PASSES, 2 * (M - P)], U8, name="w4_rest", align_bytes=64)
+        up_rows = up.rearrange("(p j) n -> p j n", j=PACK)
+        up_raw = [
+            held.tile([P, PACK, (hi - lo) * P], F32, name="up_raw%d" % lo) for lo, hi in UP_PIECES
+        ]
+
+        def load_up(u):
+            lo, hi = UP_PIECES[u]
+            nc.sync.dma_start(up_raw[u][:], up_rows[:, :, lo * P : hi * P])
+
+        nc.sync.dma_start(w4_first[:].bitcast(I32), word_rows[:, :, 0 : 2 * P].bitcast(I32))
+        load_up(0)
+        nc.sync.dma_start(places[:], offs2)
+        nc.sync.dma_start(wgo_sb[:], wgo)
+        load_up(1)
+        nc.sync.dma_start(w4_rest[:].bitcast(I32), word_rows[:, :, 2 * P : 2 * M].bitcast(I32))
+        load_up(2)
+        load_up(3)
+
+        upq = mx_operand("up", M)
+
+        def make_up(u):
+            lo, hi = UP_PIECES[u]
+            grouped = held.tile([P, (hi - lo) * P * PACK], BF16, name="up_grouped%d" % u, align_bytes=64)
+            interleave(nc.scalar.copy, grouped[:], up_raw[u][:])
+            quantize(upq, slice(lo * P, hi * P), grouped[:])
+
+        make_xg(0, x0)
+        make_down(0, d0)
+        h_passes(0)
+        make_down(1, d1)
+        make_xg(1, x1)
+        h_passes(1)
+        make_down(2, d2)
+
+        b_bank = y_psum.tile([P, P], F32, name="y_bank")
+        nc.tensor.transpose(b_bank[:], b_rows[:], ident[:])
+        b_cols = held.tile([P, TILES], F32, name="b_cols")
+        nc.scalar.copy(b_cols[:], b_bank[:, 0:TILES])
+
+        picked = ring.tile([P, PACK, S], F32, name="picked")
+        for i in range(PACK - 1):
+            gather(picked, i, x2[i])
+
+        def last_gather(c):
+            nc.vector.tensor_tensor(
+                picked[:, PACK - 1, chunk_cols(c)],
+                x2[PACK - 1][:].indirect(picks[:, chunk_offsets(c)]),
+                wgt_sb[:, chunk_cols(c)],
+                MULT,
+            )
+
+        def last_xg(c):
+            grouped = held.tile([P, CHUNK * PACK], BF16, name="xg_last%d" % c, align_bytes=64)
+            copy = nc.scalar.copy if c < 2 else nc.vector.tensor_copy
+            interleave(copy, grouped[:], picked[:, :, chunk_cols(c)])
+            quantize(xg[LAST], chunk_cols(c), grouped[:])
+            for t in range(PACK):
+                h_pass(LAST, c, t)
+
+        def make_h(c):
+            grouped = held.tile([P, CHUNK, PACK], BF16, name="h_grouped%d" % c, align_bytes=64)
+            nc.scalar.copy(grouped[:], h_banks[c][:].rearrange("p t j -> p j t"))
+            quantize(hq, chunk_cols(c), grouped[:].rearrange("p j t -> p (j t)"))
+
+        def w4_tile(a, i):
+            if i == 0:
+                return w4_first[:, a, :]
+            return w4_rest[:, a, 2 * P * (i - 1) : 2 * P * i]
+
+        def project(i, cols, offsets):
+            width = cols.stop - cols.start
+            rows = slice(i * P, (i + 1) * P)
+            bank = y_psum.tile([P, width], F32, name="y_bank")
+            for a in range(PASSES):
+                nc.tensor.matmul_mx(
+                    out=bank[:],
+                    lhsT=w4_tile(a, i).bitcast(FP4X4),
+                    lhsT_scale=w4_scale[:, a, rows],
+                    rhs=xg[a][0][:, cols].bitcast(FP8X4),
+                    rhs_scale=xg[a][1][:, cols],
+                    start=(a == 0),
+                    stop=False,
+                )
+            nc.tensor.matmul_mx(
+                out=bank[:],
+                lhsT=upq[0][:, rows].bitcast(FP8X4),
+                lhsT_scale=upq[1][:, rows],
+                rhs=hq[0][:, cols].bitcast(FP8X4),
+                rhs_scale=hq[1][:, cols],
+                start=False,
+                stop=True,
+            )
+            act = acts.tile([P, width], F32, name="act")
+            nc.scalar.activation(act[:], bank[:], SILU, bias=b_cols[:, i : i + 1])
+            nc.vector.tensor_tensor(windows[i % WINDOWS][:].indirect(offsets), act[:], wgo_sb[:, cols], MULT)
+
+        def store(i):
+            nc.sync.dma_start(out[i * P : (i + 1) * P, :], windows[i % WINDOWS][:])
+
+        for c in range(CHUNKS):
+            last_gather(c)
+        last_xg(0)
+        last_xg(1)
+        make_up(0)
+        make_h(0)
+        last_xg(2)
+        last_xg(3)
+        make_h(1)
+        for c in range(CHUNKS):
+            project(0, chunk_cols(c), places[:, chunk_offsets(c)])
+            if c + 2 < CHUNKS:
+                make_h(c + 2)
+            if c == 2:
+                make_up(1)
+        store(0)
+        make_up(2)
+        for i in range(1, TILES):
+            if i == 2:
+                make_up(3)
+            project(i, slice(0, S), places[:])
+            store(i)

@@ -26,7 +26,8 @@ TILES = M // P
 CHUNK = 128
 CHUNKS = S // CHUNK
 GROUP = 16
-WINDOWS = 4
+WINDOWS = 3
+UP_TAGS = ("xg_last0", "h_stage1", "h_stage3", "h_stage1")
 UP_PIECES = ((0, 1), (1, 2), (2, 4), (4, 8))
 
 
@@ -70,30 +71,28 @@ def tile_list_hboth_l_silu_kernel(
         nc.sync.dma_start(picks[:], offs)
         nc.sync.dma_start(wgt_sb[:], wgt)
 
+        w4_scale = held.tile([P, PASSES, M], U8, name="w4_scale", align_bytes=64)
+        b_rows = held.tile([P, P], F32, name="b_rows")
+        nc.vector.memset(b_rows[0 : P // 2, :], 0.0)
+        nc.vector.memset(w4_scale[:].bitcast(I32), 0)
         windows = [held.tile([P, T], F32, name="window%d" % w) for w in range(WINDOWS)]
         for window in windows:
             nc.vector.memset(window[:], 0.0)
-        w4_scale = held.tile([P, PASSES, M], U8, name="w4_scale", align_bytes=64)
-        nc.vector.memset(w4_scale[:].bitcast(I32), 0)
 
         ident = held.tile([P, P], F32, name="ident")
         make_identity(nc, ident[:])
-        b_rows = held.tile([P, P], F32, name="b_rows")
-        nc.scalar.activation(b_rows[:], ident[:], SILU, scale=0.0)
+        nc.scalar.activation(b_rows[P // 2 : P, :], ident[P // 2 : P, :], SILU, scale=0.0)
 
         xg = [mx_operand("xg%d" % a, S) for a in range(PASSES)]
         dn = [mx_operand("down%d" % a, R) for a in range(PASSES)]
         hq = mx_operand("h", S)
         h_banks = [h_psum.tile([P, PACK, CHUNK], F32, name="h_bank%d" % c) for c in range(CHUNKS)]
 
-        def load_x(a):
+        def load_plane(a, i):
             rows = xT[a * K_PASS : (a + 1) * K_PASS, :].rearrange("(p i) t -> p i t", i=PACK)
-            planes = []
-            for i in range(PACK):
-                plane = held.tile([P, T], F32, name="x%d_%d" % (a, i))
-                nc.sync.dma_start(plane[:], rows[:, i, :])
-                planes.append(plane)
-            return planes
+            plane = held.tile([P, T], F32, name="x%d_%d" % (a, i))
+            nc.sync.dma_start(plane[:], rows[:, i, :])
+            return plane
 
         def load_down(a):
             raw = held.tile([P, PACK, R], F32, name="down_raw%d" % a)
@@ -103,21 +102,24 @@ def tile_list_hboth_l_silu_kernel(
         def gather(picked, i, plane):
             nc.vector.tensor_tensor(picked[:, i, :], plane[:].indirect(picks[:]), wgt_sb[:], MULT)
 
-        def make_xg(a, planes):
+        def gather_pass(planes):
             picked = ring.tile([P, PACK, S], F32, name="picked")
-            for i in range(PACK):
-                gather(picked, i, planes[i])
+            for i, plane in enumerate(planes):
+                gather(picked, i, plane)
+            return picked
+
+        def round_xg(picked):
             grouped = ring.tile([P, S * PACK], BF16, name="xg_grouped", align_bytes=64)
             interleave(nc.scalar.copy, grouped[:], picked[:])
-            quantize(xg[a], slice(0, S), grouped[:])
+            return grouped
 
-        def make_down(a, raw):
+        def round_down(raw):
             grouped = ring.tile([P, R * PACK], BF16, name="down_grouped", align_bytes=64)
             nc.scalar.copy(
                 grouped[:].rearrange("p (t m j) -> p m j t", t=PACK, j=PACK),
                 raw[:].rearrange("p j (m t) -> p m j t", t=PACK),
             )
-            quantize(dn[a], slice(0, R), grouped[:])
+            return grouped
 
         def h_pass(a, c, t):
             nc.tensor.matmul_mx(
@@ -135,19 +137,7 @@ def tile_list_hboth_l_silu_kernel(
                 for c in range(CHUNKS):
                     h_pass(a, c, t)
 
-        x0 = load_x(0)
-        d0 = load_down(0)
-        d1 = load_down(1)
-        x1 = load_x(1)
-        d2 = load_down(2)
-        nc.sync.dma_start(b_rows[0:TILES, :], b.rearrange("(i p) -> i p", p=P))
-        x2 = load_x(2)
-
         scale_rows = w4_scales.rearrange("a q n -> q a n")
-        for q in range(4):
-            nc.sync.dma_start(
-                w4_scale[32 * q : 32 * q + 4, :, :].bitcast(I32), scale_rows[4 * q : 4 * q + 4, :, :].bitcast(I32)
-            )
         word_rows = w4_words.rearrange("a p n -> p a n")
         w4_first = held.tile([P, PASSES, 2 * P], U8, name="w4_first", align_bytes=64)
         w4_rest = held.tile([P, PASSES, 2 * (M - P)], U8, name="w4_rest", align_bytes=64)
@@ -160,9 +150,22 @@ def tile_list_hboth_l_silu_kernel(
             lo, hi = UP_PIECES[u]
             nc.sync.dma_start(up_raw[u][:], up_rows[:, :, lo * P : hi * P])
 
-        nc.sync.dma_start(w4_first[:].bitcast(I32), word_rows[:, :, 0 : 2 * P].bitcast(I32))
-        load_up(0)
+        x0 = [load_plane(0, 0)]
+        nc.sync.dma_start(b_rows[0:TILES, :], b.rearrange("(i p) -> i p", p=P))
+        x0.extend(load_plane(0, i) for i in range(1, PACK))
+        d0 = load_down(0)
+        x1 = [load_plane(1, i) for i in range(PACK)]
+        d1 = load_down(1)
+        x2 = [load_plane(2, i) for i in range(2)]
+        d2 = load_down(2)
         nc.sync.dma_start(places[:], offs2)
+        for q in range(4):
+            nc.sync.dma_start(
+                w4_scale[32 * q : 32 * q + 4, :, :].bitcast(I32), scale_rows[4 * q : 4 * q + 4, :, :].bitcast(I32)
+            )
+        nc.sync.dma_start(w4_first[:].bitcast(I32), word_rows[:, :, 0 : 2 * P].bitcast(I32))
+        x2.extend(load_plane(2, i) for i in range(2, PACK))
+        load_up(0)
         nc.sync.dma_start(wgo_sb[:], wgo)
         load_up(1)
         nc.sync.dma_start(w4_rest[:].bitcast(I32), word_rows[:, :, 2 * P : 2 * M].bitcast(I32))
@@ -173,26 +176,30 @@ def tile_list_hboth_l_silu_kernel(
 
         def make_up(u):
             lo, hi = UP_PIECES[u]
-            grouped = held.tile([P, (hi - lo) * P * PACK], BF16, name="up_grouped%d" % u, align_bytes=64)
+            grouped = held.tile([P, (hi - lo) * P * PACK], BF16, name="up_grouped%d" % u, tag=UP_TAGS[u], align_bytes=64)
             interleave(nc.scalar.copy, grouped[:], up_raw[u][:])
             quantize(upq, slice(lo * P, hi * P), grouped[:])
-
-        make_xg(0, x0)
-        make_down(0, d0)
-        h_passes(0)
-        make_down(1, d1)
-        make_xg(1, x1)
-        h_passes(1)
-        make_down(2, d2)
 
         b_bank = y_psum.tile([P, P], F32, name="y_bank")
         nc.tensor.transpose(b_bank[:], b_rows[:], ident[:])
         b_cols = held.tile([P, TILES], F32, name="b_cols")
         nc.scalar.copy(b_cols[:], b_bank[:, 0:TILES])
 
-        picked = ring.tile([P, PACK, S], F32, name="picked")
-        for i in range(PACK - 1):
-            gather(picked, i, x2[i])
+        xg_rounded = round_xg(gather_pass(x0))
+        down_rounded = round_down(d0)
+        picked = gather_pass(x1)
+        quantize(xg[0], slice(0, S), xg_rounded[:])
+        quantize(dn[0], slice(0, R), down_rounded[:])
+        h_passes(0)
+        xg_rounded = round_xg(picked)
+        down_rounded = round_down(d1)
+        picked = gather_pass(x2[:2])
+        quantize(xg[1], slice(0, S), xg_rounded[:])
+        quantize(dn[1], slice(0, R), down_rounded[:])
+        h_passes(1)
+        down_rounded = round_down(d2)
+
+        gather(picked, 2, x2[2])
 
         def last_gather(c):
             nc.vector.tensor_tensor(
@@ -203,7 +210,7 @@ def tile_list_hboth_l_silu_kernel(
             )
 
         def last_xg(c):
-            grouped = held.tile([P, CHUNK * PACK], BF16, name="xg_last%d" % c, align_bytes=64)
+            grouped = held.tile([P, CHUNK * PACK], BF16, name="xg_last%d" % c, tag="xg_last%d" % c, align_bytes=64)
             copy = nc.scalar.copy if c < 2 else nc.vector.tensor_copy
             interleave(copy, grouped[:], picked[:, :, chunk_cols(c)])
             quantize(xg[LAST], chunk_cols(c), grouped[:])
@@ -211,7 +218,7 @@ def tile_list_hboth_l_silu_kernel(
                 h_pass(LAST, c, t)
 
         def make_h(c):
-            grouped = held.tile([P, CHUNK, PACK], BF16, name="h_grouped%d" % c, align_bytes=64)
+            grouped = held.tile([P, CHUNK, PACK], BF16, name="h_grouped%d" % c, tag="h_stage%d" % c, align_bytes=64)
             nc.scalar.copy(grouped[:], h_banks[c][:].rearrange("p t j -> p j t"))
             quantize(hq, chunk_cols(c), grouped[:].rearrange("p j t -> p (j t)"))
 
@@ -220,20 +227,27 @@ def tile_list_hboth_l_silu_kernel(
                 return w4_first[:, a, :]
             return w4_rest[:, a, 2 * P * (i - 1) : 2 * P * i]
 
-        def project(i, cols, offsets):
+        def w4_pass(bank, a, i, cols):
+            nc.tensor.matmul_mx(
+                out=bank[:],
+                lhsT=w4_tile(a, i).bitcast(FP4X4),
+                lhsT_scale=w4_scale[:, a, i * P : (i + 1) * P],
+                rhs=xg[a][0][:, cols].bitcast(FP8X4),
+                rhs_scale=xg[a][1][:, cols],
+                start=(a == 0),
+                stop=False,
+            )
+
+        def open_sum(i, cols):
+            bank = y_psum.tile([P, cols.stop - cols.start], F32, name="y_bank")
+            for a in range(LAST):
+                w4_pass(bank, a, i, cols)
+            return bank
+
+        def project(bank, i, cols, offsets):
             width = cols.stop - cols.start
             rows = slice(i * P, (i + 1) * P)
-            bank = y_psum.tile([P, width], F32, name="y_bank")
-            for a in range(PASSES):
-                nc.tensor.matmul_mx(
-                    out=bank[:],
-                    lhsT=w4_tile(a, i).bitcast(FP4X4),
-                    lhsT_scale=w4_scale[:, a, rows],
-                    rhs=xg[a][0][:, cols].bitcast(FP8X4),
-                    rhs_scale=xg[a][1][:, cols],
-                    start=(a == 0),
-                    stop=False,
-                )
+            w4_pass(bank, LAST, i, cols)
             nc.tensor.matmul_mx(
                 out=bank[:],
                 lhsT=upq[0][:, rows].bitcast(FP8X4),
@@ -243,32 +257,36 @@ def tile_list_hboth_l_silu_kernel(
                 start=False,
                 stop=True,
             )
-            act = acts.tile([P, width], F32, name="act")
+            if i == 0 and cols.stop == S:
+                act = held.tile([P, width], F32, name="act_last_chunk", tag="h_stage1", align_bytes=64)
+            else:
+                act = acts.tile([P, width], F32, name="act")
             nc.scalar.activation(act[:], bank[:], SILU, bias=b_cols[:, i : i + 1])
             nc.vector.tensor_tensor(windows[i % WINDOWS][:].indirect(offsets), act[:], wgo_sb[:, cols], MULT)
 
         def store(i):
             nc.sync.dma_start(out[i * P : (i + 1) * P, :], windows[i % WINDOWS][:])
 
+        first_banks = [open_sum(0, chunk_cols(c)) for c in range(CHUNKS)]
         for c in range(CHUNKS):
             last_gather(c)
+            if c == 0:
+                quantize(dn[LAST], slice(0, R), down_rounded[:])
         last_xg(0)
         last_xg(1)
         make_up(0)
         make_h(0)
-        last_xg(2)
-        last_xg(3)
         make_h(1)
         for c in range(CHUNKS):
-            project(0, chunk_cols(c), places[:, chunk_offsets(c)])
+            project(first_banks[c], 0, chunk_cols(c), places[:, chunk_offsets(c)])
             if c + 2 < CHUNKS:
+                last_xg(c + 2)
                 make_h(c + 2)
             if c == 2:
                 make_up(1)
         store(0)
-        make_up(2)
         for i in range(1, TILES):
-            if i == 2:
-                make_up(3)
-            project(i, slice(0, S), places[:])
+            if i + 1 < len(UP_PIECES):
+                make_up(i + 1)
+            project(open_sum(i, slice(0, S)), i, slice(0, S), places[:])
             store(i)

@@ -95,7 +95,7 @@ def tile_list_hboth_l_silu_kernel(
             return plane
 
         def load_down(a):
-            raw = held.tile([P, PACK, R], F32, name="down_raw%d" % a)
+            raw = held.tile([P, PACK, R], F32, name="down_raw%d" % a, tag="stage%d" % a, align_bytes=64)
             nc.sync.dma_start(raw[:], down[a * K_PASS : (a + 1) * K_PASS, :].rearrange("(p j) r -> p j r", j=PACK))
             return raw
 
@@ -108,8 +108,8 @@ def tile_list_hboth_l_silu_kernel(
                 gather(picked, i, plane)
             return picked
 
-        def round_xg(picked):
-            grouped = ring.tile([P, S * PACK], BF16, name="xg_grouped", align_bytes=64)
+        def round_xg(a, picked):
+            grouped = held.tile([P, S * PACK], BF16, name="xg_grouped%d" % a, tag="stage%d" % a, align_bytes=64)
             interleave(nc.scalar.copy, grouped[:], picked[:])
             return grouped
 
@@ -156,7 +156,7 @@ def tile_list_hboth_l_silu_kernel(
         d0 = load_down(0)
         x1 = [load_plane(1, i) for i in range(PACK)]
         d1 = load_down(1)
-        x2 = [load_plane(2, i) for i in range(2)]
+        x2 = [load_plane(2, i) for i in range(PACK - 1)]
         d2 = load_down(2)
         nc.sync.dma_start(places[:], offs2)
         for q in range(4):
@@ -164,7 +164,7 @@ def tile_list_hboth_l_silu_kernel(
                 w4_scale[32 * q : 32 * q + 4, :, :].bitcast(I32), scale_rows[4 * q : 4 * q + 4, :, :].bitcast(I32)
             )
         nc.sync.dma_start(w4_first[:].bitcast(I32), word_rows[:, :, 0 : 2 * P].bitcast(I32))
-        x2.extend(load_plane(2, i) for i in range(2, PACK))
+        x2.append(load_plane(2, PACK - 1))
         load_up(0)
         nc.sync.dma_start(wgo_sb[:], wgo)
         load_up(1)
@@ -185,21 +185,20 @@ def tile_list_hboth_l_silu_kernel(
         b_cols = held.tile([P, TILES], F32, name="b_cols")
         nc.scalar.copy(b_cols[:], b_bank[:, 0:TILES])
 
-        xg_rounded = round_xg(gather_pass(x0))
+        picked = gather_pass(x0)
         down_rounded = round_down(d0)
+        xg_rounded = round_xg(0, picked)
         picked = gather_pass(x1)
-        quantize(xg[0], slice(0, S), xg_rounded[:])
         quantize(dn[0], slice(0, R), down_rounded[:])
+        quantize(xg[0], slice(0, S), xg_rounded[:])
         h_passes(0)
-        xg_rounded = round_xg(picked)
         down_rounded = round_down(d1)
-        picked = gather_pass(x2[:2])
-        quantize(xg[1], slice(0, S), xg_rounded[:])
+        xg_rounded = round_xg(1, picked)
+        picked = gather_pass(x2[: PACK - 1])
         quantize(dn[1], slice(0, R), down_rounded[:])
+        quantize(xg[1], slice(0, S), xg_rounded[:])
         h_passes(1)
         down_rounded = round_down(d2)
-
-        gather(picked, 2, x2[2])
 
         def last_gather(c):
             nc.vector.tensor_tensor(
@@ -270,8 +269,7 @@ def tile_list_hboth_l_silu_kernel(
         first_banks = [open_sum(0, chunk_cols(c)) for c in range(CHUNKS)]
         for c in range(CHUNKS):
             last_gather(c)
-            if c == 0:
-                quantize(dn[LAST], slice(0, R), down_rounded[:])
+        quantize(dn[LAST], slice(0, R), down_rounded[:])
         last_xg(0)
         last_xg(1)
         make_up(0)

from contextlib import ExitStack

import concourse.mybir as mybir
from concourse.masks import make_identity

K, M, T, S, R = 1536, 1024, 1024, 512, 512
FLOPS = 2 * S * (K * M + K * R + R * M)

F32 = mybir.dt.float32
BF16 = mybir.dt.bfloat16
I32 = mybir.dt.int32
U32 = mybir.dt.uint32
U16 = mybir.dt.uint16
U8 = mybir.dt.uint8
FP8X4 = mybir.dt.float8_e4m3fn_x4
FP4X4 = mybir.dt.float4_e2m1fn_x4
MULT = mybir.AluOpType.mult
SILU = mybir.ActivationFunctionType.Silu

P = 128
PACK = 4
K_PASS = P * PACK
PASSES = K // K_PASS
LAST = PASSES - 1
TILES = M // P
CHUNK = 128
CHUNKS = S // CHUNK
GROUP = 16
WINDOWS = 3
UP_TAGS = ("xg_last0", "h_stage1", "h_stage3", "h_stage1")
UP_PIECES = ((0, 1), (1, 2), (2, 4), (4, 8))


def tile_list_hboth_l_silu_kernel(
    tc, xT, w4_words, w4_scales, down, up, wgt, b, wgo, offs, offs2, out
):
    nc = tc.nc

    with ExitStack() as ctx:
        held = ctx.enter_context(tc.tile_pool(name="held", bufs=1))
        ring = ctx.enter_context(tc.tile_pool(name="ring", bufs=2))
        acts = ctx.enter_context(tc.tile_pool(name="acts", bufs=3))
        h_psum = ctx.enter_context(tc.psum_pool(name="h_psum", bufs=1))
        y_psum = ctx.enter_context(tc.psum_pool(name="y_psum", bufs=4))

        def mx_operand(name, width):
            codes = held.tile([P, width], U32, name=name + "_codes", align_bytes=64)
            scales = held.tile([P, width], U8, name=name + "_scales", align_bytes=64)
            return codes, scales

        def quantize(operand, cols, grouped):
            codes, scales = operand
            nc.vector.quantize_mx(out=codes[:, cols].bitcast(FP8X4), scales=scales[:, cols], in_=grouped)

        def interleave(copy, grouped, rows):
            copy(
                grouped.rearrange("p (c i t) -> p c t i", i=4, t=PACK),
                rows.rearrange("p t (c i) -> p c t i", i=4),
            )

        def chunk_cols(c):
            return slice(c * CHUNK, (c + 1) * CHUNK)

        def chunk_offsets(c):
            return slice(c * CHUNK // GROUP, (c + 1) * CHUNK // GROUP)

        picks = held.tile([P, S // GROUP], U16, name="picks")
        places = held.tile([P, S // GROUP], U16, name="places")
        wgt_sb = held.tile([P, S], F32, name="wgt_sb")
        wgo_sb = held.tile([P, S], F32, name="wgo_sb")
        nc.sync.dma_start(picks[:], offs)
        nc.sync.dma_start(wgt_sb[:], wgt)

        w4_scale = held.tile([P, PASSES, M], U8, name="w4_scale", align_bytes=64)
        b_rows = held.tile([P, P], F32, name="b_rows")
        nc.vector.memset(b_rows[0 : P // 2, :], 0.0)
        nc.vector.memset(w4_scale[:].bitcast(I32), 0)
        windows = [held.tile([P, T], F32, name="window%d" % w) for w in range(WINDOWS)]
        for window in windows:
            nc.vector.memset(window[:], 0.0)

        ident = held.tile([P, P], F32, name="ident")
        make_identity(nc, ident[:])
        nc.scalar.activation(b_rows[P // 2 : P, :], ident[P // 2 : P, :], SILU, scale=0.0)

        xg = [mx_operand("xg%d" % a, S) for a in range(PASSES)]
        dn = [mx_operand("down%d" % a, R) for a in range(PASSES)]
        hq = mx_operand("h", S)
        h_banks = [h_psum.tile([P, PACK, CHUNK], F32, name="h_bank%d" % c) for c in range(CHUNKS)]

        def load_plane(a, i):
            rows = xT[a * K_PASS : (a + 1) * K_PASS, :].rearrange("(p i) t -> p i t", i=PACK)
            plane = held.tile([P, T], F32, name="x%d_%d" % (a, i))
            nc.sync.dma_start(plane[:], rows[:, i, :])
            return plane

        def load_down(a):
            raw = held.tile([P, PACK, R], F32, name="down_raw%d" % a, tag="stage%d" % a, align_bytes=64)
            nc.sync.dma_start(raw[:], down[a * K_PASS : (a + 1) * K_PASS, :].rearrange("(p j) r -> p j r", j=PACK))
            return raw

        def gather(picked, i, plane):
            nc.vector.tensor_tensor(picked[:, i, :], plane[:].indirect(picks[:]), wgt_sb[:], MULT)

        def gather_pass(planes):
            picked = ring.tile([P, PACK, S], F32, name="picked")
            for i, plane in enumerate(planes):
                gather(picked, i, plane)
            return picked

        def round_xg(a, picked):
            grouped = held.tile([P, S * PACK], BF16, name="xg_grouped%d" % a, tag="stage%d" % a, align_bytes=64)
            interleave(nc.scalar.copy, grouped[:], picked[:])
            return grouped

        def round_down(raw):
            grouped = ring.tile([P, R * PACK], BF16, name="down_grouped", align_bytes=64)
            nc.scalar.copy(
                grouped[:].rearrange("p (t m j) -> p m j t", t=PACK, j=PACK),
                raw[:].rearrange("p j (m t) -> p m j t", t=PACK),
            )
            return grouped

        def h_pass(a, c, t):
            nc.tensor.matmul_mx(
                out=h_banks[c][:, t, :],
                lhsT=dn[a][0][:, t * P : (t + 1) * P].bitcast(FP8X4),
                lhsT_scale=dn[a][1][:, t * P : (t + 1) * P],
                rhs=xg[a][0][:, chunk_cols(c)].bitcast(FP8X4),
                rhs_scale=xg[a][1][:, chunk_cols(c)],
                start=(a == 0 and t == 0),
                stop=(a == LAST and t == PACK - 1),
            )

        def h_passes(a):
            for t in range(PACK):
                for c in range(CHUNKS):
                    h_pass(a, c, t)

        scale_rows = w4_scales.rearrange("a q n -> q a n")
        word_rows = w4_words.rearrange("a p n -> p a n")
        w4_first = held.tile([P, PASSES, 2 * P], U8, name="w4_first", align_bytes=64)
        w4_rest = held.tile([P, PASSES, 2 * (M - P)], U8, name="w4_rest", align_bytes=64)
        up_rows = up.rearrange("(p j) n -> p j n", j=PACK)
        up_raw = [
            held.tile([P, PACK, (hi - lo) * P], F32, name="up_raw%d" % lo) for lo, hi in UP_PIECES
        ]

        def load_up(u):
            lo, hi = UP_PIECES[u]
            nc.sync.dma_start(up_raw[u][:], up_rows[:, :, lo * P : hi * P])

        x0 = [load_plane(0, 0)]
        nc.sync.dma_start(b_rows[0:TILES, :], b.rearrange("(i p) -> i p", p=P))
        x0.extend(load_plane(0, i) for i in range(1, PACK))
        d0 = load_down(0)
        x1 = [load_plane(1, i) for i in range(PACK)]
        d1 = load_down(1)
        x2 = [load_plane(2, i) for i in range(PACK - 1)]
        d2 = load_down(2)
        nc.sync.dma_start(places[:], offs2)
        for q in range(4):
            nc.sync.dma_start(
                w4_scale[32 * q : 32 * q + 4, :, :].bitcast(I32), scale_rows[4 * q : 4 * q + 4, :, :].bitcast(I32)
            )
        nc.sync.dma_start(w4_first[:].bitcast(I32), word_rows[:, :, 0 : 2 * P].bitcast(I32))
        x2.append(load_plane(2, PACK - 1))
        load_up(0)
        nc.sync.dma_start(wgo_sb[:], wgo)
        load_up(1)
        nc.sync.dma_start(w4_rest[:].bitcast(I32), word_rows[:, :, 2 * P : 2 * M].bitcast(I32))
        load_up(2)
        load_up(3)

        upq = mx_operand("up", M)

        def make_up(u):
            lo, hi = UP_PIECES[u]
            grouped = held.tile([P, (hi - lo) * P * PACK], BF16, name="up_grouped%d" % u, tag=UP_TAGS[u], align_bytes=64)
            interleave(nc.scalar.copy, grouped[:], up_raw[u][:])
            quantize(upq, slice(lo * P, hi * P), grouped[:])

        b_bank = y_psum.tile([P, P], F32, name="y_bank")
        nc.tensor.transpose(b_bank[:], b_rows[:], ident[:])
        b_cols = held.tile([P, TILES], F32, name="b_cols")
        nc.scalar.copy(b_cols[:], b_bank[:, 0:TILES])

        picked = gather_pass(x0)
        down_rounded = round_down(d0)
        xg_rounded = round_xg(0, picked)
        picked = gather_pass(x1)
        quantize(dn[0], slice(0, R), down_rounded[:])
        quantize(xg[0], slice(0, S), xg_rounded[:])
        h_passes(0)
        down_rounded = round_down(d1)
        xg_rounded = round_xg(1, picked)
        picked = gather_pass(x2[: PACK - 1])
        quantize(dn[1], slice(0, R), down_rounded[:])
        quantize(xg[1], slice(0, S), xg_rounded[:])
        h_passes(1)
        down_rounded = round_down(d2)

        def last_gather(c):
            nc.vector.tensor_tensor(
                picked[:, PACK - 1, chunk_cols(c)],
                x2[PACK - 1][:].indirect(picks[:, chunk_offsets(c)]),
                wgt_sb[:, chunk_cols(c)],
                MULT,
            )

        def last_xg(c):
            grouped = held.tile([P, CHUNK * PACK], BF16, name="xg_last%d" % c, tag="xg_last%d" % c, align_bytes=64)
            copy = nc.scalar.copy if c < 2 else nc.vector.tensor_copy
            interleave(copy, grouped[:], picked[:, :, chunk_cols(c)])
            quantize(xg[LAST], chunk_cols(c), grouped[:])
            for t in range(PACK):
                h_pass(LAST, c, t)

        def make_h(c):
            grouped = held.tile([P, CHUNK, PACK], BF16, name="h_grouped%d" % c, tag="h_stage%d" % c, align_bytes=64)
            nc.scalar.copy(grouped[:], h_banks[c][:].rearrange("p t j -> p j t"))
            quantize(hq, chunk_cols(c), grouped[:].rearrange("p j t -> p (j t)"))

        def w4_tile(a, i):
            if i == 0:
                return w4_first[:, a, :]
            return w4_rest[:, a, 2 * P * (i - 1) : 2 * P * i]

        def w4_pass(bank, a, i, cols):
            nc.tensor.matmul_mx(
                out=bank[:],
                lhsT=w4_tile(a, i).bitcast(FP4X4),
                lhsT_scale=w4_scale[:, a, i * P : (i + 1) * P],
                rhs=xg[a][0][:, cols].bitcast(FP8X4),
                rhs_scale=xg[a][1][:, cols],
                start=(a == 0),
                stop=False,
            )

        def open_sum(i, cols):
            bank = y_psum.tile([P, cols.stop - cols.start], F32, name="y_bank")
            for a in range(LAST):
                w4_pass(bank, a, i, cols)
            return bank

        def project(bank, i, cols, offsets):
            width = cols.stop - cols.start
            rows = slice(i * P, (i + 1) * P)
            w4_pass(bank, LAST, i, cols)
            nc.tensor.matmul_mx(
                out=bank[:],
                lhsT=upq[0][:, rows].bitcast(FP8X4),
                lhsT_scale=upq[1][:, rows],
                rhs=hq[0][:, cols].bitcast(FP8X4),
                rhs_scale=hq[1][:, cols],
                start=False,
                stop=True,
            )
            if i == 0 and cols.stop == S:
                act = held.tile([P, width], F32, name="act_last_chunk", tag="h_stage1", align_bytes=64)
            else:
                act = acts.tile([P, width], F32, name="act")
            nc.scalar.activation(act[:], bank[:], SILU, bias=b_cols[:, i : i + 1])
            nc.vector.tensor_tensor(windows[i % WINDOWS][:].indirect(offsets), act[:], wgo_sb[:, cols], MULT)

        def store(i):
            nc.sync.dma_start(out[i * P : (i + 1) * P, :], windows[i % WINDOWS][:])

        first_banks = [open_sum(0, chunk_cols(c)) for c in range(CHUNKS)]
        for c in range(CHUNKS):
            last_gather(c)
        quantize(dn[LAST], slice(0, R), down_rounded[:])
        last_xg(0)
        last_xg(1)
        make_up(0)
        make_h(0)
        make_h(1)
        for c in range(CHUNKS):
            project(first_banks[c], 0, chunk_cols(c), places[:, chunk_offsets(c)])
            if c + 2 < CHUNKS:
                last_xg(c + 2)
                make_h(c + 2)
            if c == 2:
                make_up(1)
        store(0)
        for i in range(1, TILES):
            if i + 1 < len(UP_PIECES):
                make_up(i + 1)
            project(open_sum(i, slice(0, S)), i, slice(0, S), places[:])
            store(i)
